import numpy as np
import ml_dtypes


def mxq(x, axis, fmt="e4m3"):
    dtype, down = {"e4m3": (ml_dtypes.float8_e4m3fn, 7), "e5m2": (ml_dtypes.float8_e5m2, 14)}[fmt]
    v = np.moveaxis(np.asarray(x, np.float32).astype(ml_dtypes.bfloat16).astype(np.float64), axis, -1)
    blocks = v.reshape(v.shape[:-1] + (-1, 32))
    amax = np.abs(blocks).max(-1, keepdims=True)
    byte = np.maximum(np.where(amax > 0, np.frexp(amax)[1] - 1 + 127, 0) - down, 1)
    scale = np.exp2(byte - 127.0)
    codes = (blocks / scale).astype(np.float32).astype(dtype).astype(np.float64)
    return np.moveaxis((codes * scale).reshape(v.shape), -1, axis)


WIDE = False


def mx_kscale(k):
    if not WIDE:
        return np.ones(k)
    levels = np.array([10, -10, 5, -5, 0])
    if k % 512:
        return np.exp2(np.random.permutation(np.resize(levels, k // 32))).repeat(32)
    a = np.empty((k // 512, 16))
    for p in range(k // 512):
        a[p, :8] = np.random.permutation(np.resize(levels, 8))
        for g in range(8):
            far = levels[np.abs(levels - a[p, g]) >= 10]
            a[p, g + 8] = far[np.random.randint(len(far))]
    return np.exp2(a.ravel()).repeat(32)


BF16 = ml_dtypes.bfloat16


def bf(x):
    return np.asarray(x, np.float32).astype(BF16)


def f64(x):
    return np.asarray(x).astype(np.float64)

def planes(Y):
    n, m = Y.shape
    b = f64(bf(Y)).reshape(n // 32, 32, m)
    amax = np.abs(b).max(1)
    byte = np.clip(np.where(amax > 0, np.frexp(amax)[1] - 1 + 127 - 7, 1), 1, 254)
    codes = (b * np.exp2(127.0 - byte)[:, None, :]).reshape(n, m).astype(np.float32).astype(ml_dtypes.float8_e4m3fn).view(np.uint8)
    words = codes.reshape(n // 512, 128, 4, m).transpose(0, 1, 3, 2)
    return np.ascontiguousarray(words), np.ascontiguousarray(byte.astype(np.uint8).reshape(n // 512, 16, m))


B, NS, NT, D, V = 4, 512, 512, 1024, 512
TEMPERATURE = 0.8
POWER = 0.8


def setup_inputs():
    s, t = mx_kscale(D), mx_kscale(NT)
    return {
        "x": bf(np.random.standard_normal((B, NS, D)) * s),
        "y": bf(np.random.standard_normal((B, NT, D)) / np.sqrt(D) / s),
        "p": bf(np.random.uniform(0.5, 1.5, (B, NS))),
        "q": bf(np.random.uniform(0.5, 1.5, (B, NT))),
        "g": bf(np.random.standard_normal((B, NT)) * t),
        "ys": bf(np.random.standard_normal((B, NS, V))),
        "yt": bf(np.random.standard_normal((B, NT, V)) / np.sqrt(NT) / t[:, None]),
    }


def core(x, y, p, q, g, ys, yt):
    cs = mxq(f64(x), 2, "e4m3") @ mxq(f64(y), 2, "e4m3").transpose(0, 2, 1)
    k = np.exp(cs / TEMPERATURE)
    a = (f64(p) / np.mean(k, axis=2)) ** POWER
    bb = (f64(q) / np.mean(k * a[:, :, None], axis=1)) ** POWER
    tr = a[:, :, None] * k * bb[:, None, :]
    mass = np.mean(tr, axis=2)
    tg = tr * f64(g)[:, None, :]
    return (mxq(tg, 2, "e4m3") @ mxq(f64(yt), 1, "e4m3")) - mass[:, :, None] * f64(ys)


def reference(x, y, p, q, g, ys, yt):
    R_out = core(x, y, p, q, g, ys, yt)
    words, scales = planes(np.moveaxis(R_out, 1, 0).reshape(512, -1))
    return R_out, words, scales

@@ -1,0 +1,351 @@
+from contextlib import ExitStack
+
+import concourse.mybir as mybir
+from concourse.masks import make_identity
+
+B, NS, NT, D, V = 4, 512, 512, 1024, 512
+TEMPERATURE = 0.8
+POWER = 0.8
+FLOPS = 2 * B * NS * NT * (D + V)
+
+F32 = mybir.dt.float32
+BF16 = mybir.dt.bfloat16
+I32 = mybir.dt.int32
+U32 = mybir.dt.uint32
+U8 = mybir.dt.uint8
+FP8X4 = mybir.dt.float8_e4m3fn_x4
+ALU = mybir.AluOpType
+ACT = mybir.ActivationFunctionType
+
+P = 128
+PACK = 4
+K_PASS = P * PACK
+PASSES = D // K_PASS
+HALF = 256
+assert NS == NT == K_PASS
+
+LOADS = [("y",1), ("x",1), ("yt",0), ("y",2), ("x",2), ("ys",0), ("yt",1), ("y",3), ("x",3), ("ys",1), ("yt",2), ("ys",2), ("yt",3), ("ys",3)]
+ORDER = [
+    ("Ty", 0, 0, 0), ("Ty", 0, 1, 0), ("Ty", 0, 2, 0), ("Ty", 0, 3, 0), ("Cy", 0, 0, 1),
+    ("Tx", 0, 0, 0), ("Tx", 0, 1, 0), ("Tx", 0, 2, 0), ("Tx", 0, 3, 0), ("Cy", 0, 1, 1),
+    ("Cy", 0, 2, 0), ("Cy", 0, 3, 0), ("Qy", 0, 0, 0), ("Qy", 0, 1, 0), ("Cx", 0, 0, 0),
+    ("Cx", 0, 1, 0), ("Cx", 0, 2, 0), ("Qx", 0, 0, 0), ("Cx", 0, 3, 0), ("Qx", 0, 1, 0),
+    ("M1", 0, 0, 0), ("M1", 0, 1, 0), ("M1", 0, 2, 0), ("M1", 0, 3, 0), ("Ty", 1, 0, 0),
+    ("Ty", 1, 1, 0), ("E", 0, 0, 0), ("E", 0, 1, 0), ("E", 0, 2, 0), ("E", 0, 3, 0),
+    ("Ty", 1, 2, 0), ("GA", 0, 0, 0), ("Ty", 1, 3, 0), ("Cy", 1, 0, 1), ("Cy", 1, 1, 1),
+    ("Cy", 1, 2, 1), ("Cy", 1, 3, 0), ("Tx", 1, 0, 0), ("Tx", 1, 1, 0), ("Tx", 1, 2, 0),
+    ("Tx", 1, 3, 0), ("KA", 0, 0, 1), ("KA", 0, 1, 0), ("KA", 0, 2, 0), ("KA", 0, 3, 0),
+    ("Cx", 1, 0, 0), ("Qy", 1, 0, 0), ("Qy", 1, 1, 0), ("TK", 0, 0, 0), ("Cx", 1, 1, 0),
+    ("TK", 0, 1, 0), ("TK", 0, 2, 0), ("TK", 0, 3, 0), ("Cx", 1, 2, 0), ("Qx", 1, 0, 0),
+    ("Cx", 1, 3, 0), ("Qx", 1, 1, 0), ("CK", 0, 0, 0), ("CK", 0, 1, 0), ("CK", 0, 2, 0),
+    ("M1", 1, 0, 0), ("CK", 0, 3, 0), ("M1", 1, 1, 0), ("M1", 1, 2, 0), ("M1", 1, 3, 0),
+    ("Ty", 2, 0, 0), ("YI", 0, 0, 1), ("Ty", 2, 1, 0), ("E", 1, 0, 0), ("E", 1, 1, 0),
+    ("E", 1, 2, 0), ("E", 1, 3, 0), ("YI", 0, 1, 1), ("Ty", 2, 2, 0), ("GB", 0, 0, 0),
+    ("Ty", 2, 3, 0), ("CM", 0, 0, 0), ("Cy", 2, 0, 1), ("QV", 0, 0, 0), ("GA", 1, 0, 0),
+    ("Cy", 2, 1, 0), ("MS", 0, 0, 0), ("Cy", 2, 2, 0), ("Cy", 2, 3, 0), ("Tx", 2, 0, 0),
+    ("Tx", 2, 1, 0), ("Tx", 2, 2, 0), ("Tx", 2, 3, 0), ("TG", 0, 0, 0), ("TG", 0, 1, 0),
+    ("KA", 1, 0, 1), ("KA", 1, 1, 1), ("KA", 1, 2, 0), ("KA", 1, 3, 0), ("Cx", 2, 0, 0),
+    ("QT", 0, 0, 0), ("Qy", 2, 0, 0), ("Qy", 2, 1, 0), ("Cx", 2, 1, 0), ("TK", 1, 0, 0),
+    ("TK", 1, 1, 0), ("YI", 1, 0, 1), ("QT", 0, 1, 0), ("Cx", 2, 2, 0), ("TK", 1, 2, 0),
+    ("TK", 1, 3, 0), ("Qx", 2, 0, 0), ("M2", 0, 0, 0), ("YI", 1, 1, 1), ("Cx", 2, 3, 0),
+    ("M2", 0, 1, 0), ("CK", 1, 0, 0), ("Qx", 2, 1, 0), ("CK", 1, 1, 0), ("M2", 0, 2, 0),
+    ("M1", 2, 0, 0), ("CK", 1, 2, 0), ("CK", 1, 3, 0), ("M1", 2, 1, 0), ("M1", 2, 2, 0),
+    ("M2", 0, 3, 0), ("M1", 2, 3, 0), ("O", 0, 0, 0), ("O", 0, 1, 0), ("Ty", 3, 0, 0),
+    ("O", 0, 2, 0), ("O", 0, 3, 0), ("E", 2, 0, 0), ("E", 2, 1, 0), ("E", 2, 2, 0),
+    ("E", 2, 3, 0), ("Ty", 3, 1, 0), ("OI", 0, 0, 1), ("Ty", 3, 2, 0), ("QV", 1, 0, 0),
+    ("Ty", 3, 3, 0), ("OI", 0, 1, 0), ("Cy", 3, 0, 0), ("Cy", 3, 1, 0), ("Cy", 3, 2, 0),
+    ("Cy", 3, 3, 0), ("GB", 1, 0, 0), ("CM", 1, 0, 0), ("Tx", 3, 0, 0), ("Tx", 3, 1, 0),
+    ("Tx", 3, 2, 0), ("Tx", 3, 3, 0), ("YI", 2, 0, 1), ("GA", 2, 0, 0), ("MS", 1, 0, 0),
+    ("YI", 2, 1, 1), ("TG", 1, 0, 0), ("Cx", 3, 0, 0), ("SO", 0, 0, 0), ("TG", 1, 1, 0),
+    ("QO", 0, 0, 0), ("KA", 2, 0, 1), ("KA", 2, 1, 1), ("KA", 2, 2, 0), ("KA", 2, 3, 0),
+    ("SO", 0, 1, 0), ("Cx", 3, 1, 0), ("Qy", 3, 0, 0), ("SW", 0, 0, 0), ("Qy", 3, 1, 0),
+    ("QO", 0, 1, 0), ("SW", 0, 1, 0), ("SO", 0, 2, 0), ("QT", 1, 0, 0), ("Cx", 3, 2, 0),
+    ("TK", 2, 0, 0), ("TK", 2, 1, 0), ("Qx", 3, 0, 0), ("TK", 2, 2, 0), ("SO", 0, 3, 0),
+    ("TK", 2, 3, 0), ("Cx", 3, 3, 0), ("M2", 1, 0, 0), ("QT", 1, 1, 0), ("CK", 2, 0, 0),
+    ("Qx", 3, 1, 0), ("M1", 3, 0, 0), ("CK", 2, 1, 0), ("M1", 3, 1, 0), ("M2", 1, 1, 0),
+    ("CK", 2, 2, 0), ("CK", 2, 3, 0), ("M1", 3, 2, 0), ("M1", 3, 3, 0), ("M2", 1, 2, 0),
+    ("YI", 3, 0, 1), ("E", 3, 0, 0), ("E", 3, 1, 0), ("E", 3, 2, 0), ("E", 3, 3, 0),
+    ("M2", 1, 3, 0), ("YI", 3, 1, 0), ("QV", 2, 0, 0), ("O", 1, 0, 0), ("O", 1, 1, 0),
+    ("O", 1, 2, 0), ("O", 1, 3, 0), ("OI", 1, 0, 1), ("GB", 2, 0, 0), ("CM", 2, 0, 0),
+    ("OI", 1, 1, 1), ("GA", 3, 0, 0), ("MS", 2, 0, 0), ("SO", 1, 0, 0), ("SO", 1, 1, 0),
+    ("TG", 2, 0, 0), ("KA", 3, 0, 0), ("KA", 3, 1, 0), ("KA", 3, 2, 0), ("KA", 3, 3, 0),
+    ("QO", 1, 0, 0), ("TK", 3, 0, 0), ("TG", 2, 1, 0), ("SO", 1, 2, 0), ("TK", 3, 1, 0),
+    ("TK", 3, 2, 0), ("QT", 2, 0, 0), ("TK", 3, 3, 0), ("QO", 1, 1, 0), ("CK", 3, 0, 0),
+    ("SO", 1, 3, 0), ("CK", 3, 1, 0), ("CK", 3, 2, 0), ("M2", 2, 0, 0), ("CK", 3, 3, 0),
+    ("QT", 2, 1, 0), ("SW", 1, 0, 0), ("SW", 1, 1, 0), ("M2", 2, 1, 0), ("QV", 3, 0, 0),
+    ("M2", 2, 2, 0), ("M2", 2, 3, 0), ("O", 2, 0, 0), ("O", 2, 1, 0), ("O", 2, 2, 0),
+    ("O", 2, 3, 0), ("GB", 3, 0, 0), ("CM", 3, 0, 0), ("OI", 2, 0, 1), ("OI", 2, 1, 1),
+    ("MS", 3, 0, 0), ("SO", 2, 0, 0), ("SO", 2, 1, 0), ("SO", 2, 2, 0), ("TG", 3, 0, 0),
+    ("QO", 2, 0, 0), ("QT", 3, 0, 0), ("SO", 2, 3, 0), ("TG", 3, 1, 0), ("QO", 2, 1, 0),
+    ("M2", 3, 0, 0), ("M2", 3, 1, 0), ("QT", 3, 1, 0), ("M2", 3, 2, 0), ("M2", 3, 3, 0),
+    ("SW", 2, 0, 0), ("SW", 2, 1, 0), ("O", 3, 0, 0), ("O", 3, 1, 0), ("O", 3, 2, 0),
+    ("O", 3, 3, 0), ("OI", 3, 0, 0), ("OI", 3, 1, 0), ("SO", 3, 0, 0), ("SO", 3, 1, 0),
+    ("SO", 3, 2, 0), ("SO", 3, 3, 0), ("QO", 3, 0, 0), ("QO", 3, 1, 0), ("SW", 3, 0, 0),
+    ("SW", 3, 1, 0),
+]
+
+
+def tile_unbalancedsinkhorngainedsumdifference_kernel(tc, x, y, p, q, g, ys, yt, out_0, out_1, out_2):
+    nc = tc.nc
+    with ExitStack() as ctx:
+        const = ctx.enter_context(tc.tile_pool(name="const", bufs=1))
+        inputs = ctx.enter_context(tc.tile_pool(name="inputs", bufs=B))
+        work = ctx.enter_context(tc.tile_pool(name="work", bufs=2))
+        small = ctx.enter_context(tc.tile_pool(name="small", bufs=B))
+        banks = ctx.enter_context(tc.psum_pool(name="banks", bufs=7))
+        mass_bank = ctx.enter_context(tc.psum_pool(name="mass_bank", bufs=1))
+        ctx.enter_context(tc.manual_schedule())
+
+        st = [dict() for b in range(B)]
+        sources = {"x": x, "y": y, "yt": yt, "ys": ys}
+
+        def get(b, name, pool, shape, dtype):
+            if name not in st[b]:
+                st[b][name] = pool.tile(shape, dtype, name=name, align_bytes=64)
+            return st[b][name]
+
+        def load(name, b):
+            rows = sources[name][b].rearrange("(p t) d -> p t d", t=PACK)
+            dst = get(b, name, inputs, [P, PACK, rows.shape[2]], BF16)
+            step = PACK if name in ("yt", "ys") else (1 if b == 0 else 2)
+            for t in range(0, PACK, step):
+                nc.sync.dma_start(out=dst[:, t : t + step, :], in_=rows[:, t : t + step, :])
+
+        ident = const.tile([P, P], F32)
+        make_identity(nc, ident[:])
+        facs = const.tile([P, B, 2, PACK], F32)
+        nc.gpsimd.memset(facs[:], -1.0)
+        expo = const.tile([P, PACK], F32)
+        nc.scalar.activation(out=expo[:], in_=facs[:, 0, 0, :], func=ACT.Copy, scale=POWER)
+        load("y", 0)
+        load("x", 0)
+        pq = const.tile([P, 2, B, PACK], BF16)
+        g_sb = const.tile([P, B, PACK], BF16)
+        pq_inv = const.tile([P, 2, B, PACK], F32)
+        nc.sync.dma_start(out=pq[:, 0], in_=p.rearrange("b (p t) -> p b t", t=PACK))
+        nc.sync.dma_start(out=pq[:, 1], in_=q.rearrange("b (p t) -> p b t", t=PACK))
+        nc.sync.dma_start(out=g_sb[:], in_=g.rearrange("b (p t) -> p b t", t=PACK))
+        for name, b in LOADS:
+            load(name, b)
+        nc.gpsimd.tensor_scalar(out=facs[:, :, 1, :], in0=g_sb[:], scalar1=float(NT), scalar2=0.0, op0=ALU.mult, op1=ALU.add)
+        out_scales = const.tile([P, B * V], U8, align_bytes=64)
+
+        def copy_on(alt, out, in_):
+            if alt:
+                nc.vector.tensor_copy(out=out, in_=in_)
+            else:
+                nc.scalar.copy(out=out, in_=in_)
+
+        def turn(name, b, t):
+            bank = banks.tile([P, PASSES, 2, P], F32, name="bank")
+            st[b]["turned", name, t] = bank
+            words = st[b][name][:, t, :].bitcast(F32)
+            for c in range(PASSES):
+                for u in range(2):
+                    nc.tensor.transpose(bank[:, c, u, :], words[:, 256 * c + u : 256 * (c + 1) : 2], ident[:])
+
+        def s_Ty(b, t, alt):
+            turn("y", b, t)
+
+        def s_Tx(b, t, alt):
+            turn("x", b, t)
+
+        def s_Cy(b, t, alt):
+            yg = get(b, "yg", work, [P, PASSES, PACK, P * PACK], BF16)
+            out = yg[:, :, t, :].bitcast(F32).rearrange("p c (r u) -> p c r u", u=2)
+            copy_on(alt, out, st[b]["turned", "y", t][:].rearrange("p c u r -> p c r u"))
+
+        def s_Cx(b, t, alt):
+            xg = get(b, "xg", work, [P, PACK, PASSES, P * PACK], BF16)
+            out = xg[:, t, :, :].bitcast(F32).rearrange("p c (r u) -> p c r u", u=2)
+            copy_on(alt, out, st[b]["turned", "x", t][:].rearrange("p c u r -> p c r u"))
+
+        def s_Qy(b, c, alt):
+            codes = get(b, "yq", work, [P, PASSES, NT], U32)
+            scales = get(b, "ysc", work, [P, PASSES, NT], U8)
+            nc.vector.quantize_mx(
+                out=codes[:, c, :].bitcast(FP8X4), scales=scales[:, c, :], in_=st[b]["yg"][:, c].rearrange("p t n -> p (t n)")
+            )
+
+        def s_Qx(b, h, alt):
+            codes = get(b, "xq", work, [P, 2, 2 * PASSES * P], U32)
+            scales = get(b, "xsc", work, [P, 2, 2 * PASSES * P], U8)
+            nc.vector.quantize_mx(
+                out=codes[:, h, :].bitcast(FP8X4),
+                scales=scales[:, h, :],
+                in_=st[b]["xg"][:, 2 * h : 2 * h + 2].rearrange("p t c n -> p (t c n)"),
+            )
+            if b == 0 and h == 1:
+                nc.vector.reciprocal(out=pq_inv[:], in_=pq[:])
+
+        def s_M1(b, t, alt):
+            s = st[b]
+            bank = banks.tile([P, NT], F32, name="bank")
+            s["score", t] = bank
+            for c in range(PASSES):
+                cols = slice(P * (PASSES * (t % 2) + c), P * (PASSES * (t % 2) + c + 1))
+                nc.tensor.matmul_mx(
+                    out=bank[:],
+                    lhsT=s["xq"][:, t // 2, cols].bitcast(FP8X4),
+                    lhsT_scale=s["xsc"][:, t // 2, cols],
+                    rhs=s["yq"][:, c, :].bitcast(FP8X4),
+                    rhs_scale=s["ysc"][:, c, :],
+                    start=(c == 0),
+                    stop=(c == PASSES - 1),
+                )
+
+        def s_E(b, t, alt):
+            k = get(b, "k", work, [P, PACK, NT], F32)
+            rs = get(b, "rs", small, [P, PACK], F32)
+            nc.scalar.activation(
+                out=k[:, t, :], in_=st[b]["score", t][:], func=ACT.Exp, scale=1.0 / TEMPERATURE, accum_out=rs[:, t : t + 1]
+            )
+
+        def s_GA(b, t, alt):
+            ratio = get(b, "row_ratio", small, [P, PACK], F32)
+            a = get(b, "a", small, [P, PACK], F32)
+            nc.gpsimd.tensor_tensor(out=ratio[:], in0=st[b]["rs"][:], in1=pq_inv[:, 0, b, :], op=ALU.mult)
+            nc.gpsimd.tensor_tensor(out=a[:], in0=ratio[:], in1=expo[:], op=ALU.pow)
+
+        def s_KA(b, t, alt):
+            s = st[b]
+            if alt:
+                nc.scalar.activation(out=s["k"][:, t, :], in_=s["k"][:, t, :], func=ACT.Copy, scale=s["a"][:, t : t + 1])
+            else:
+                nc.vector.tensor_scalar(
+                    out=s["k"][:, t, :], in0=s["k"][:, t, :], scalar1=s["a"][:, t : t + 1], scalar2=None, op0=ALU.mult
+                )
+
+        def s_TK(b, tj, alt):
+            bank = banks.tile([P, PACK, P], F32, name="bank")
+            st[b]["kturned", tj] = bank
+            for ti in range(PACK):
+                nc.tensor.transpose(bank[:, ti, :], st[b]["k"][:, ti, P * tj : P * (tj + 1)], ident[:])
+
+        def s_CK(b, tj, alt):
+            kt = get(b, "kt", work, [P, PACK, NS], F32)
+            cs = get(b, "cs", small, [P, PACK], F32)
+            nc.scalar.activation(
+                out=kt[:, tj, :],
+                in_=st[b]["kturned", tj][:].rearrange("p t r -> p (t r)"),
+                func=ACT.Copy,
+                scale=NT ** (POWER - 1.0),
+                accum_out=cs[:, tj : tj + 1],
+            )
+
+        def s_GB(b, t, alt):
+            ratio = get(b, "col_ratio", small, [P, PACK], F32)
+            bb = get(b, "bb", small, [P, PACK], F32)
+            cf = get(b, "cf", small, [P, 2, PACK], F32)
+            nc.gpsimd.tensor_tensor(out=ratio[:], in0=st[b]["cs"][:], in1=pq_inv[:, 1, b, :], op=ALU.mult)
+            nc.gpsimd.tensor_tensor(out=bb[:], in0=ratio[:], in1=expo[:], op=ALU.pow)
+            nc.gpsimd.tensor_tensor(
+                out=cf[:], in0=facs[:, b], in1=bb[:].unsqueeze(1).to_broadcast([P, 2, PACK]), op=ALU.mult
+            )
+
+        def s_CM(b, t, alt):
+            bank = banks.tile([P, PACK], F32, name="bank")
+            st[b]["gain"] = bank
+            nc.tensor.matmul(out=bank[:], lhsT=ident[:], rhs=st[b]["cf"][:, 1, :], start=True, stop=True)
+
+        def s_TG(b, h, alt):
+            tg = get(b, "tg", work, [P, NS, PACK], BF16)
+            cols = slice(HALF * h, HALF * (h + 1))
+            nc.vector.tensor_tensor(
+                out=tg[:, cols, :],
+                in0=st[b]["kt"][:, :, cols].rearrange("p t i -> p i t"),
+                in1=st[b]["gain"][:].unsqueeze(1).to_broadcast([P, HALF, PACK]),
+                op=ALU.mult,
+            )
+
+        def s_QT(b, h, alt):
+            codes = get(b, "tq", work, [P, NS], U32)
+            scales = get(b, "tsc", work, [P, NS], U8)
+            cols = slice(HALF * h, HALF * (h + 1))
+            nc.vector.quantize_mx(
+                out=codes[:, cols].bitcast(FP8X4), scales=scales[:, cols], in_=st[b]["tg"][:, cols, :].rearrange("p n t -> p (n t)")
+            )
+
+        def s_YI(b, h, alt):
+            s = st[b]
+            get(b, "ytg", work, [P, V, PACK], BF16)
+            cols = slice(HALF * h, HALF * (h + 1))
+            copy_on(alt, s["ytg"][:, cols, :], s["yt"][:, :, cols].rearrange("p t v -> p v t"))
+
+        def s_QV(b, t, alt):
+            codes = get(b, "vq", work, [P, V], U32)
+            scales = get(b, "vsc", work, [P, V], U8)
+            nc.vector.quantize_mx(out=codes[:].bitcast(FP8X4), scales=scales[:], in_=st[b]["ytg"][:].rearrange("p n t -> p (n t)"))
+
+        def s_MS(b, t, alt):
+            s = st[b]
+            s["m"] = mass_bank.tile([P, PACK], F32, name="neg_mass")
+            for ti in range(PACK):
+                for tj in range(PACK):
+                    nc.tensor.matmul(
+                        out=s["m"][:, ti : ti + 1],
+                        lhsT=s["kt"][:, tj, P * ti : P * (ti + 1)],
+                        rhs=s["cf"][:, 0, tj : tj + 1],
+                        start=(tj == 0),
+                        stop=(tj == PACK - 1),
+                    )
+
+        def s_M2(b, t, alt):
+            s = st[b]
+            bank = banks.tile([P, V], F32, name="bank")
+            s["sum", t] = bank
+            cols = slice(P * t, P * (t + 1))
+            nc.tensor.matmul_mx(
+                out=bank[:],
+                lhsT=s["tq"][:, cols].bitcast(FP8X4),
+                lhsT_scale=s["tsc"][:, cols],
+                rhs=s["vq"][:].bitcast(FP8X4),
+                rhs_scale=s["vsc"][:],
+                start=True,
+                stop=True,
+            )
+
+        def s_O(b, t, alt):
+            s = st[b]
+            o = get(b, "o", work, [P, PACK, V], F32)
+            nc.vector.scalar_tensor_tensor(
+                out=o[:, t, :], in0=s["ys"][:, t, :], scalar=s["m"][:, t : t + 1], in1=s["sum", t][:], op0=ALU.mult, op1=ALU.add
+            )
+
+        def s_SO(b, t, alt):
+            rows = out_0[b].rearrange("(p t) v -> p t v", t=PACK)
+            nc.sync.dma_start(out=rows[:, t, :], in_=st[b]["o"][:, t, :])
+
+        def s_OI(b, h, alt):
+            s = st[b]
+            get(b, "og", work, [P, V, PACK], BF16)
+            cols = slice(HALF * h, HALF * (h + 1))
+            copy_on(not alt, s["og"][:, cols, :], s["o"][:, :, cols].rearrange("p t v -> p v t"))
+
+        def s_QO(b, h, alt):
+            codes = get(b, "oq", work, [P, V], U32)
+            cols = slice(HALF * h, HALF * (h + 1))
+            nc.vector.quantize_mx(
+                out=codes[:, cols].bitcast(FP8X4),
+                scales=out_scales[:, V * b + HALF * h : V * b + HALF * (h + 1)],
+                in_=st[b]["og"][:, cols, :].rearrange("p n t -> p (n t)"),
+            )
+
+        def s_SW(b, h, alt):
+            words = out_1[0].rearrange("p m t -> p (m t)").bitcast(I32)
+            nc.sync.dma_start(
+                out=words[:, V * b + HALF * h : V * b + HALF * (h + 1)], in_=st[b]["oq"][:, HALF * h : HALF * (h + 1)].bitcast(I32)
+            )
+
+        steps = {
+            "Ty": s_Ty, "Tx": s_Tx, "Cy": s_Cy, "Cx": s_Cx, "Qy": s_Qy, "Qx": s_Qx, "M1": s_M1, "E": s_E, "GA": s_GA,
+            "KA": s_KA, "TK": s_TK, "CK": s_CK, "GB": s_GB, "CM": s_CM, "TG": s_TG, "QT": s_QT, "YI": s_YI, "QV": s_QV,
+            "MS": s_MS, "M2": s_M2, "O": s_O, "SO": s_SO, "OI": s_OI, "QO": s_QO, "SW": s_SW,
+        }
+        for name, b, t, alt in ORDER:
+            steps[name](b, t, alt)
+        for quad in range(4):
+            nc.scalar.dma_start(
+                out=out_2[0, 4 * quad : 4 * quad + 4, :].bitcast(I32),
+                in_=out_scales[32 * quad : 32 * quad + 4, :].bitcast(I32),
+            )

@@ -24,64 +24,67 @@ PASSES = D // K_PASS
 HALF = 256
 assert NS == NT == K_PASS
 
-LOADS = [("y",1), ("x",1), ("yt",0), ("y",2), ("x",2), ("ys",0), ("yt",1), ("y",3), ("x",3), ("ys",1), ("yt",2), ("ys",2), ("yt",3), ("ys",3)]
+LOADS = [("yt",0), ("y",1), ("x",1), ("yt",1), ("yt",2), ("y",2), ("x",2), ("yt",3), ("y",3), ("x",3), ("ys",0), ("ys",1), ("ys",2), ("ys",3)]
 ORDER = [
-    ("Ty", 0, 0, 0), ("Ty", 0, 1, 0), ("Ty", 0, 2, 0), ("Ty", 0, 3, 0), ("Cy", 0, 0, 1),
-    ("Tx", 0, 0, 0), ("Tx", 0, 1, 0), ("Tx", 0, 2, 0), ("Tx", 0, 3, 0), ("Cy", 0, 1, 1),
+    ("Ty", 0, 0, 0), ("Ty", 0, 1, 0), ("Ty", 0, 2, 0), ("Ty", 0, 3, 0), ("Tx", 0, 0, 0),
+    ("Tx", 0, 1, 0), ("Tx", 0, 2, 0), ("Tx", 0, 3, 0), ("Cy", 0, 0, 1), ("Cy", 0, 1, 1),
     ("Cy", 0, 2, 0), ("Cy", 0, 3, 0), ("Qy", 0, 0, 0), ("Qy", 0, 1, 0), ("Cx", 0, 0, 0),
     ("Cx", 0, 1, 0), ("Cx", 0, 2, 0), ("Qx", 0, 0, 0), ("Cx", 0, 3, 0), ("Qx", 0, 1, 0),
     ("M1", 0, 0, 0), ("M1", 0, 1, 0), ("M1", 0, 2, 0), ("M1", 0, 3, 0), ("Ty", 1, 0, 0),
-    ("Ty", 1, 1, 0), ("E", 0, 0, 0), ("E", 0, 1, 0), ("E", 0, 2, 0), ("E", 0, 3, 0),
-    ("Ty", 1, 2, 0), ("GA", 0, 0, 0), ("Ty", 1, 3, 0), ("Cy", 1, 0, 1), ("Cy", 1, 1, 1),
-    ("Cy", 1, 2, 1), ("Cy", 1, 3, 0), ("Tx", 1, 0, 0), ("Tx", 1, 1, 0), ("Tx", 1, 2, 0),
-    ("Tx", 1, 3, 0), ("KA", 0, 0, 1), ("KA", 0, 1, 0), ("KA", 0, 2, 0), ("KA", 0, 3, 0),
-    ("Cx", 1, 0, 0), ("Qy", 1, 0, 0), ("Qy", 1, 1, 0), ("TK", 0, 0, 0), ("Cx", 1, 1, 0),
-    ("TK", 0, 1, 0), ("TK", 0, 2, 0), ("TK", 0, 3, 0), ("Cx", 1, 2, 0), ("Qx", 1, 0, 0),
-    ("Cx", 1, 3, 0), ("Qx", 1, 1, 0), ("CK", 0, 0, 0), ("CK", 0, 1, 0), ("CK", 0, 2, 0),
-    ("M1", 1, 0, 0), ("CK", 0, 3, 0), ("M1", 1, 1, 0), ("M1", 1, 2, 0), ("M1", 1, 3, 0),
-    ("Ty", 2, 0, 0), ("YI", 0, 0, 1), ("Ty", 2, 1, 0), ("E", 1, 0, 0), ("E", 1, 1, 0),
-    ("E", 1, 2, 0), ("E", 1, 3, 0), ("YI", 0, 1, 1), ("Ty", 2, 2, 0), ("GB", 0, 0, 0),
-    ("Ty", 2, 3, 0), ("CM", 0, 0, 0), ("Cy", 2, 0, 1), ("QV", 0, 0, 0), ("GA", 1, 0, 0),
-    ("Cy", 2, 1, 0), ("MS", 0, 0, 0), ("Cy", 2, 2, 0), ("Cy", 2, 3, 0), ("Tx", 2, 0, 0),
-    ("Tx", 2, 1, 0), ("Tx", 2, 2, 0), ("Tx", 2, 3, 0), ("TG", 0, 0, 0), ("TG", 0, 1, 0),
-    ("KA", 1, 0, 1), ("KA", 1, 1, 1), ("KA", 1, 2, 0), ("KA", 1, 3, 0), ("Cx", 2, 0, 0),
-    ("QT", 0, 0, 0), ("Qy", 2, 0, 0), ("Qy", 2, 1, 0), ("Cx", 2, 1, 0), ("TK", 1, 0, 0),
-    ("TK", 1, 1, 0), ("YI", 1, 0, 1), ("QT", 0, 1, 0), ("Cx", 2, 2, 0), ("TK", 1, 2, 0),
-    ("TK", 1, 3, 0), ("Qx", 2, 0, 0), ("M2", 0, 0, 0), ("YI", 1, 1, 1), ("Cx", 2, 3, 0),
-    ("M2", 0, 1, 0), ("CK", 1, 0, 0), ("Qx", 2, 1, 0), ("CK", 1, 1, 0), ("M2", 0, 2, 0),
-    ("M1", 2, 0, 0), ("CK", 1, 2, 0), ("CK", 1, 3, 0), ("M1", 2, 1, 0), ("M1", 2, 2, 0),
-    ("M2", 0, 3, 0), ("M1", 2, 3, 0), ("O", 0, 0, 0), ("O", 0, 1, 0), ("Ty", 3, 0, 0),
-    ("O", 0, 2, 0), ("O", 0, 3, 0), ("E", 2, 0, 0), ("E", 2, 1, 0), ("E", 2, 2, 0),
-    ("E", 2, 3, 0), ("Ty", 3, 1, 0), ("OI", 0, 0, 1), ("Ty", 3, 2, 0), ("QV", 1, 0, 0),
-    ("Ty", 3, 3, 0), ("OI", 0, 1, 0), ("Cy", 3, 0, 0), ("Cy", 3, 1, 0), ("Cy", 3, 2, 0),
-    ("Cy", 3, 3, 0), ("GB", 1, 0, 0), ("CM", 1, 0, 0), ("Tx", 3, 0, 0), ("Tx", 3, 1, 0),
-    ("Tx", 3, 2, 0), ("Tx", 3, 3, 0), ("YI", 2, 0, 1), ("GA", 2, 0, 0), ("MS", 1, 0, 0),
-    ("YI", 2, 1, 1), ("TG", 1, 0, 0), ("Cx", 3, 0, 0), ("SO", 0, 0, 0), ("TG", 1, 1, 0),
-    ("QO", 0, 0, 0), ("KA", 2, 0, 1), ("KA", 2, 1, 1), ("KA", 2, 2, 0), ("KA", 2, 3, 0),
-    ("SO", 0, 1, 0), ("Cx", 3, 1, 0), ("Qy", 3, 0, 0), ("SW", 0, 0, 0), ("Qy", 3, 1, 0),
-    ("QO", 0, 1, 0), ("SW", 0, 1, 0), ("SO", 0, 2, 0), ("QT", 1, 0, 0), ("Cx", 3, 2, 0),
-    ("TK", 2, 0, 0), ("TK", 2, 1, 0), ("Qx", 3, 0, 0), ("TK", 2, 2, 0), ("SO", 0, 3, 0),
-    ("TK", 2, 3, 0), ("Cx", 3, 3, 0), ("M2", 1, 0, 0), ("QT", 1, 1, 0), ("CK", 2, 0, 0),
-    ("Qx", 3, 1, 0), ("M1", 3, 0, 0), ("CK", 2, 1, 0), ("M1", 3, 1, 0), ("M2", 1, 1, 0),
-    ("CK", 2, 2, 0), ("CK", 2, 3, 0), ("M1", 3, 2, 0), ("M1", 3, 3, 0), ("M2", 1, 2, 0),
-    ("YI", 3, 0, 1), ("E", 3, 0, 0), ("E", 3, 1, 0), ("E", 3, 2, 0), ("E", 3, 3, 0),
-    ("M2", 1, 3, 0), ("YI", 3, 1, 0), ("QV", 2, 0, 0), ("O", 1, 0, 0), ("O", 1, 1, 0),
-    ("O", 1, 2, 0), ("O", 1, 3, 0), ("OI", 1, 0, 1), ("GB", 2, 0, 0), ("CM", 2, 0, 0),
-    ("OI", 1, 1, 1), ("GA", 3, 0, 0), ("MS", 2, 0, 0), ("SO", 1, 0, 0), ("SO", 1, 1, 0),
-    ("TG", 2, 0, 0), ("KA", 3, 0, 0), ("KA", 3, 1, 0), ("KA", 3, 2, 0), ("KA", 3, 3, 0),
-    ("QO", 1, 0, 0), ("TK", 3, 0, 0), ("TG", 2, 1, 0), ("SO", 1, 2, 0), ("TK", 3, 1, 0),
-    ("TK", 3, 2, 0), ("QT", 2, 0, 0), ("TK", 3, 3, 0), ("QO", 1, 1, 0), ("CK", 3, 0, 0),
-    ("SO", 1, 3, 0), ("CK", 3, 1, 0), ("CK", 3, 2, 0), ("M2", 2, 0, 0), ("CK", 3, 3, 0),
-    ("QT", 2, 1, 0), ("SW", 1, 0, 0), ("SW", 1, 1, 0), ("M2", 2, 1, 0), ("QV", 3, 0, 0),
-    ("M2", 2, 2, 0), ("M2", 2, 3, 0), ("O", 2, 0, 0), ("O", 2, 1, 0), ("O", 2, 2, 0),
-    ("O", 2, 3, 0), ("GB", 3, 0, 0), ("CM", 3, 0, 0), ("OI", 2, 0, 1), ("OI", 2, 1, 1),
-    ("MS", 3, 0, 0), ("SO", 2, 0, 0), ("SO", 2, 1, 0), ("SO", 2, 2, 0), ("TG", 3, 0, 0),
-    ("QO", 2, 0, 0), ("QT", 3, 0, 0), ("SO", 2, 3, 0), ("TG", 3, 1, 0), ("QO", 2, 1, 0),
-    ("M2", 3, 0, 0), ("M2", 3, 1, 0), ("QT", 3, 1, 0), ("M2", 3, 2, 0), ("M2", 3, 3, 0),
-    ("SW", 2, 0, 0), ("SW", 2, 1, 0), ("O", 3, 0, 0), ("O", 3, 1, 0), ("O", 3, 2, 0),
-    ("O", 3, 3, 0), ("OI", 3, 0, 0), ("OI", 3, 1, 0), ("SO", 3, 0, 0), ("SO", 3, 1, 0),
-    ("SO", 3, 2, 0), ("SO", 3, 3, 0), ("QO", 3, 0, 0), ("QO", 3, 1, 0), ("SW", 3, 0, 0),
-    ("SW", 3, 1, 0),
+    ("Ty", 1, 1, 0), ("Ty", 1, 2, 0), ("Ty", 1, 3, 0), ("YI", 0, 0, 1), ("YI", 0, 1, 1),
+    ("QV", 0, 0, 0), ("E", 0, 0, 0), ("E", 0, 1, 0), ("E", 0, 2, 0), ("E", 0, 3, 0),
+    ("Cy", 1, 0, 1), ("Cy", 1, 1, 1), ("Cy", 1, 2, 1), ("GA", 0, 0, 0), ("Cy", 1, 3, 0),
+    ("KA", 0, 0, 1), ("KA", 0, 1, 0), ("KA", 0, 2, 0), ("KA", 0, 3, 0), ("Tx", 1, 0, 0),
+    ("Tx", 1, 1, 0), ("Tx", 1, 2, 0), ("Tx", 1, 3, 0), ("YI", 1, 0, 1), ("Cx", 1, 0, 0),
+    ("YI", 1, 1, 1), ("Cx", 1, 1, 0), ("Cx", 1, 2, 0), ("Cx", 1, 3, 0), ("TK", 0, 0, 0),
+    ("TK", 0, 1, 0), ("TK", 0, 2, 0), ("TK", 0, 3, 0), ("Ty", 2, 0, 0), ("Ty", 2, 1, 0),
+    ("Ty", 2, 2, 0), ("Ty", 2, 3, 0), ("YI", 2, 0, 1), ("YI", 2, 1, 1), ("CK", 0, 0, 0),
+    ("CK", 0, 1, 0), ("CK", 0, 2, 0), ("Tx", 2, 0, 0), ("CK", 0, 3, 0), ("Tx", 2, 1, 0),
+    ("Tx", 2, 2, 0), ("Tx", 2, 3, 0), ("Qy", 1, 0, 0), ("Qx", 1, 0, 0), ("Qy", 1, 1, 0),
+    ("Qx", 1, 1, 0), ("Cx", 2, 0, 1), ("GB", 0, 0, 0), ("Cy", 2, 0, 0), ("Cx", 2, 1, 1),
+    ("Cy", 2, 1, 0), ("Cy", 2, 2, 0), ("Cx", 2, 2, 1), ("Qx", 2, 0, 0), ("Cy", 2, 3, 0),
+    ("Cx", 2, 3, 0), ("Qx", 2, 1, 0), ("M1", 1, 0, 0), ("M1", 1, 1, 0), ("M1", 1, 2, 0),
+    ("M1", 1, 3, 0), ("QV", 2, 0, 0), ("Ty", 3, 0, 0), ("Ty", 3, 1, 0), ("Ty", 3, 2, 0),
+    ("Ty", 3, 3, 0), ("Qy", 2, 0, 0), ("Qy", 2, 1, 0), ("M1", 2, 0, 0), ("M1", 2, 1, 0),
+    ("M1", 2, 2, 0), ("M1", 2, 3, 0), ("TR", 0, 0, 1), ("TR", 0, 1, 1), ("TR", 0, 2, 0),
+    ("TR", 0, 3, 0), ("E", 1, 0, 0), ("E", 1, 1, 0), ("E", 1, 2, 0), ("E", 1, 3, 0),
+    ("GA", 1, 0, 0), ("Tx", 3, 0, 0), ("Tx", 3, 1, 0), ("Tx", 3, 2, 0), ("Tx", 3, 3, 0),
+    ("QV", 1, 0, 0), ("TG", 0, 0, 0), ("TG", 0, 1, 0), ("TS", 0, 0, 0), ("Cy", 3, 0, 0),
+    ("Cy", 3, 1, 0), ("Cy", 3, 2, 0), ("KA", 1, 0, 0), ("Cy", 3, 3, 0), ("E", 2, 0, 0),
+    ("KA", 1, 1, 0), ("QT", 0, 0, 0), ("Qy", 3, 0, 0), ("KA", 1, 2, 0), ("E", 2, 1, 0),
+    ("KA", 1, 3, 0), ("E", 2, 2, 0), ("QT", 0, 1, 0), ("Qy", 3, 1, 0), ("E", 2, 3, 0),
+    ("Cx", 3, 0, 1), ("Cx", 3, 1, 0), ("Cx", 3, 2, 0), ("RS", 0, 0, 0), ("Cx", 3, 3, 0),
+    ("TK", 1, 0, 0), ("TK", 1, 1, 0), ("TK", 1, 2, 0), ("TK", 1, 3, 0), ("Qx", 3, 0, 0),
+    ("GA", 2, 0, 0), ("Qx", 3, 1, 0), ("CK", 1, 0, 0), ("CK", 1, 1, 0), ("CK", 1, 2, 0),
+    ("CK", 1, 3, 0), ("M2", 0, 0, 0), ("M2", 0, 1, 0), ("M2", 0, 2, 0), ("M2", 0, 3, 0),
+    ("M1", 3, 0, 0), ("M1", 3, 1, 0), ("M1", 3, 2, 0), ("M1", 3, 3, 0), ("KA", 2, 0, 1),
+    ("KA", 2, 1, 1), ("KA", 2, 2, 1), ("KA", 2, 3, 0), ("O", 0, 0, 0), ("O", 0, 1, 0),
+    ("O", 0, 2, 0), ("O", 0, 3, 0), ("GB", 1, 0, 0), ("E", 3, 0, 0), ("TK", 2, 0, 0),
+    ("TK", 2, 1, 0), ("TK", 2, 2, 0), ("TK", 2, 3, 0), ("E", 3, 1, 0), ("E", 3, 2, 0),
+    ("E", 3, 3, 0), ("TR", 1, 0, 0), ("TR", 1, 1, 0), ("TR", 1, 2, 0), ("TR", 1, 3, 0),
+    ("YI", 3, 0, 1), ("YI", 3, 1, 1), ("TG", 1, 0, 0), ("TG", 1, 1, 0), ("TS", 1, 0, 0),
+    ("CK", 2, 0, 0), ("CK", 2, 1, 0), ("CK", 2, 2, 0), ("RS", 1, 0, 1), ("CK", 2, 3, 0),
+    ("QT", 1, 0, 0), ("QT", 1, 1, 0), ("GA", 3, 0, 0), ("KA", 3, 0, 1), ("KA", 3, 1, 1),
+    ("KA", 3, 2, 0), ("GB", 2, 0, 0), ("KA", 3, 3, 0), ("M2", 1, 0, 0), ("M2", 1, 1, 0),
+    ("M2", 1, 2, 0), ("M2", 1, 3, 0), ("SO", 0, 0, 0), ("SO", 0, 1, 0), ("SO", 0, 2, 0),
+    ("SO", 0, 3, 0), ("O", 1, 0, 0), ("O", 1, 1, 0), ("O", 1, 2, 0), ("O", 1, 3, 0),
+    ("SO", 1, 0, 0), ("SO", 1, 1, 0), ("SO", 1, 2, 0), ("SO", 1, 3, 0), ("TR", 2, 0, 0),
+    ("TR", 2, 1, 0), ("TR", 2, 2, 0), ("TR", 2, 3, 0), ("QV", 3, 0, 0), ("TG", 2, 0, 0),
+    ("OI", 0, 0, 1), ("TK", 3, 0, 0), ("TK", 3, 1, 0), ("TK", 3, 2, 0), ("TK", 3, 3, 0),
+    ("CK", 3, 0, 0), ("TG", 2, 1, 0), ("CK", 3, 1, 0), ("CK", 3, 2, 0), ("CK", 3, 3, 0),
+    ("OI", 0, 1, 1), ("GB", 3, 0, 0), ("QT", 2, 0, 0), ("QT", 2, 1, 0), ("TS", 2, 0, 0),
+    ("QO", 0, 0, 0), ("QO", 0, 1, 0), ("RS", 2, 0, 1), ("M2", 2, 0, 0), ("M2", 2, 1, 0),
+    ("M2", 2, 2, 0), ("M2", 2, 3, 0), ("TR", 3, 0, 1), ("TR", 3, 1, 1), ("TR", 3, 2, 1),
+    ("TR", 3, 3, 1), ("TS", 3, 0, 0), ("O", 2, 0, 0), ("O", 2, 1, 0), ("O", 2, 2, 0),
+    ("O", 2, 3, 0), ("TG", 3, 0, 0), ("TG", 3, 1, 0), ("QT", 3, 0, 0), ("QT", 3, 1, 0),
+    ("OI", 1, 0, 1), ("M2", 3, 0, 0), ("M2", 3, 1, 0), ("M2", 3, 2, 0), ("M2", 3, 3, 0),
+    ("OI", 1, 1, 1), ("QO", 1, 0, 0), ("QO", 1, 1, 0), ("SW", 0, 0, 0), ("SO", 2, 0, 0),
+    ("SO", 2, 1, 0), ("SO", 2, 2, 0), ("SO", 2, 3, 0), ("SW", 0, 1, 0), ("RS", 3, 0, 1),
+    ("OI", 2, 0, 1), ("SW", 1, 0, 0), ("O", 3, 0, 0), ("O", 3, 1, 0), ("O", 3, 2, 0),
+    ("O", 3, 3, 0), ("OI", 2, 1, 1), ("SW", 1, 1, 0), ("SO", 3, 0, 0), ("SO", 3, 1, 0),
+    ("SO", 3, 2, 0), ("SO", 3, 3, 0), ("OI", 3, 0, 1), ("OI", 3, 1, 0), ("QO", 2, 0, 0),
+    ("QO", 2, 1, 0), ("QO", 3, 0, 0), ("QO", 3, 1, 0), ("SW", 2, 0, 0), ("SW", 2, 1, 0),
+    ("SW", 3, 0, 0), ("SW", 3, 1, 0),
 ]
 
 
@@ -93,7 +96,8 @@ def tile_unbalancedsinkhorngainedsumdifference_kernel(tc, x, y, p, q, g, ys, yt,
         work = ctx.enter_context(tc.tile_pool(name="work", bufs=2))
         small = ctx.enter_context(tc.tile_pool(name="small", bufs=B))
         banks = ctx.enter_context(tc.psum_pool(name="banks", bufs=7))
-        mass_bank = ctx.enter_context(tc.psum_pool(name="mass_bank", bufs=1))
+        gain_bank = ctx.enter_context(tc.psum_pool(name="gain_bank", bufs=1))
+        feats = ctx.enter_context(tc.tile_pool(name="feats", bufs=3))
         ctx.enter_context(tc.manual_schedule())
 
         st = [dict() for b in range(B)]
@@ -106,17 +110,17 @@ def tile_unbalancedsinkhorngainedsumdifference_kernel(tc, x, y, p, q, g, ys, yt,
 
         def load(name, b):
             rows = sources[name][b].rearrange("(p t) d -> p t d", t=PACK)
-            dst = get(b, name, inputs, [P, PACK, rows.shape[2]], BF16)
+            dst = get(b, name, inputs if name in ("yt", "ys") else feats, [P, PACK, rows.shape[2]], BF16)
             step = PACK if name in ("yt", "ys") else (1 if b == 0 else 2)
             for t in range(0, PACK, step):
                 nc.sync.dma_start(out=dst[:, t : t + step, :], in_=rows[:, t : t + step, :])
 
         ident = const.tile([P, P], F32)
         make_identity(nc, ident[:])
-        facs = const.tile([P, B, 2, PACK], F32)
-        nc.gpsimd.memset(facs[:], -1.0)
+        neg_one = const.tile([P, PACK], F32)
+        nc.gpsimd.memset(neg_one[:], -1.0)
         expo = const.tile([P, PACK], F32)
-        nc.scalar.activation(out=expo[:], in_=facs[:, 0, 0, :], func=ACT.Copy, scale=POWER)
+        nc.scalar.activation(out=expo[:], in_=neg_one[:], func=ACT.Copy, scale=POWER)
         load("y", 0)
         load("x", 0)
         pq = const.tile([P, 2, B, PACK], BF16)
@@ -127,7 +131,11 @@ def tile_unbalancedsinkhorngainedsumdifference_kernel(tc, x, y, p, q, g, ys, yt,
         nc.sync.dma_start(out=g_sb[:], in_=g.rearrange("b (p t) -> p b t", t=PACK))
         for name, b in LOADS:
             load(name, b)
-        nc.gpsimd.tensor_scalar(out=facs[:, :, 1, :], in0=g_sb[:], scalar1=float(NT), scalar2=0.0, op0=ALU.mult, op1=ALU.add)
+        g_fac = const.tile([P, B * PACK], F32)
+        nc.gpsimd.tensor_scalar(
+            out=g_fac[:], in0=g_sb[:].rearrange("p b t -> p (b t)"), scalar1=-float(NT), scalar2=0.0, op0=ALU.mult, op1=ALU.add
+        )
+        gains = gain_bank.tile([P, B, PACK], F32)
         out_scales = const.tile([P, B * V], U8, align_bytes=64)
 
         def copy_on(alt, out, in_):
@@ -177,6 +185,9 @@ def tile_unbalancedsinkhorngainedsumdifference_kernel(tc, x, y, p, q, g, ys, yt,
             )
             if b == 0 and h == 1:
                 nc.vector.reciprocal(out=pq_inv[:], in_=pq[:])
+                nc.gpsimd.tensor_scalar(
+                    out=pq_inv[:, 1], in0=pq_inv[:, 1], scalar1=-1.0, scalar2=0.0, op0=ALU.mult, op1=ALU.add
+                )
 
         def s_M1(b, t, alt):
             s = st[b]
@@ -217,6 +228,8 @@ def tile_unbalancedsinkhorngainedsumdifference_kernel(tc, x, y, p, q, g, ys, yt,
                 )
 
         def s_TK(b, tj, alt):
+            if b == 0 and tj == 0:
+                nc.tensor.matmul(out=gains[:].rearrange("p b t -> p (b t)"), lhsT=ident[:], rhs=g_fac[:], start=True, stop=True)
             bank = banks.tile([P, PACK, P], F32, name="bank")
             st[b]["kturned", tj] = bank
             for ti in range(PACK):
@@ -229,24 +242,48 @@ def tile_unbalancedsinkhorngainedsumdifference_kernel(tc, x, y, p, q, g, ys, yt,
                 out=kt[:, tj, :],
                 in_=st[b]["kturned", tj][:].rearrange("p t r -> p (t r)"),
                 func=ACT.Copy,
-                scale=NT ** (POWER - 1.0),
+                scale=-(NT ** (POWER - 1.0)),
                 accum_out=cs[:, tj : tj + 1],
             )
 
         def s_GB(b, t, alt):
             ratio = get(b, "col_ratio", small, [P, PACK], F32)
             bb = get(b, "bb", small, [P, PACK], F32)
-            cf = get(b, "cf", small, [P, 2, PACK], F32)
             nc.gpsimd.tensor_tensor(out=ratio[:], in0=st[b]["cs"][:], in1=pq_inv[:, 1, b, :], op=ALU.mult)
             nc.gpsimd.tensor_tensor(out=bb[:], in0=ratio[:], in1=expo[:], op=ALU.pow)
-            nc.gpsimd.tensor_tensor(
-                out=cf[:], in0=facs[:, b], in1=bb[:].unsqueeze(1).to_broadcast([P, 2, PACK]), op=ALU.mult
-            )
 
-        def s_CM(b, t, alt):
-            bank = banks.tile([P, PACK], F32, name="bank")
-            st[b]["gain"] = bank
-            nc.tensor.matmul(out=bank[:], lhsT=ident[:], rhs=st[b]["cf"][:, 1, :], start=True, stop=True)
+        def s_TR(b, t, alt):
+            s = st[b]
+            if alt:
+                nc.scalar.activation(out=s["kt"][:, t, :], in_=s["kt"][:, t, :], func=ACT.Copy, scale=s["bb"][:, t : t + 1])
+            else:
+                nc.vector.tensor_scalar(
+                    out=s["kt"][:, t, :], in0=s["kt"][:, t, :], scalar1=s["bb"][:, t : t + 1], scalar2=None, op0=ALU.mult
+                )
+
+        def s_TS(b, t, alt):
+            bank = banks.tile([P, PACK, P], F32, name="bank")
+            st[b]["partial"] = bank
+            for ti in range(PACK):
+                for tj in range(PACK):
+                    nc.tensor.matmul(
+                        out=bank[:, ti, :],
+                        lhsT=st[b]["kt"][:, tj, P * ti : P * (ti + 1)],
+                        rhs=ident[:],
+                        start=(tj == 0),
+                        stop=(tj == PACK - 1),
+                        is_transpose=True,
+                    )
+
+        def s_RS(b, t, alt):
+            m = get(b, "m", small, [P, PACK], F32)
+            bank = st[b]["partial"]
+            if alt:
+                junk = get(b, "junk", small, [P, PACK, P], F32)
+                for ti in range(PACK):
+                    nc.scalar.activation(out=junk[:, ti, :], in_=bank[:, ti, :], func=ACT.Copy, accum_out=m[:, ti : ti + 1])
+            else:
+                nc.vector.tensor_reduce(out=m[:], in_=bank[:], axis=mybir.AxisListType.X, op=ALU.add)
 
         def s_TG(b, h, alt):
             tg = get(b, "tg", work, [P, NS, PACK], BF16)
@@ -254,7 +291,7 @@ def tile_unbalancedsinkhorngainedsumdifference_kernel(tc, x, y, p, q, g, ys, yt,
             nc.vector.tensor_tensor(
                 out=tg[:, cols, :],
                 in0=st[b]["kt"][:, :, cols].rearrange("p t i -> p i t"),
-                in1=st[b]["gain"][:].unsqueeze(1).to_broadcast([P, HALF, PACK]),
+                in1=gains[:, b, :].unsqueeze(1).to_broadcast([P, HALF, PACK]),
                 op=ALU.mult,
             )
 
@@ -273,22 +310,9 @@ def tile_unbalancedsinkhorngainedsumdifference_kernel(tc, x, y, p, q, g, ys, yt,
             copy_on(alt, s["ytg"][:, cols, :], s["yt"][:, :, cols].rearrange("p t v -> p v t"))
 
         def s_QV(b, t, alt):
-            codes = get(b, "vq", work, [P, V], U32)
-            scales = get(b, "vsc", work, [P, V], U8)
+            codes = get(b, "vq", small, [P, V], U32)
+            scales = get(b, "vsc", small, [P, V], U8)
             nc.vector.quantize_mx(out=codes[:].bitcast(FP8X4), scales=scales[:], in_=st[b]["ytg"][:].rearrange("p n t -> p (n t)"))
-
-        def s_MS(b, t, alt):
-            s = st[b]
-            s["m"] = mass_bank.tile([P, PACK], F32, name="neg_mass")
-            for ti in range(PACK):
-                for tj in range(PACK):
-                    nc.tensor.matmul(
-                        out=s["m"][:, ti : ti + 1],
-                        lhsT=s["kt"][:, tj, P * ti : P * (ti + 1)],
-                        rhs=s["cf"][:, 0, tj : tj + 1],
-                        start=(tj == 0),
-                        stop=(tj == PACK - 1),
-                    )
 
         def s_M2(b, t, alt):
             s = st[b]
@@ -339,8 +363,8 @@ def tile_unbalancedsinkhorngainedsumdifference_kernel(tc, x, y, p, q, g, ys, yt,
 
         steps = {
             "Ty": s_Ty, "Tx": s_Tx, "Cy": s_Cy, "Cx": s_Cx, "Qy": s_Qy, "Qx": s_Qx, "M1": s_M1, "E": s_E, "GA": s_GA,
-            "KA": s_KA, "TK": s_TK, "CK": s_CK, "GB": s_GB, "CM": s_CM, "TG": s_TG, "QT": s_QT, "YI": s_YI, "QV": s_QV,
-            "MS": s_MS, "M2": s_M2, "O": s_O, "SO": s_SO, "OI": s_OI, "QO": s_QO, "SW": s_SW,
+            "KA": s_KA, "TK": s_TK, "CK": s_CK, "GB": s_GB, "TR": s_TR, "TG": s_TG, "QT": s_QT, "YI": s_YI, "QV": s_QV,
+            "TS": s_TS, "RS": s_RS, "M2": s_M2, "O": s_O, "SO": s_SO, "OI": s_OI, "QO": s_QO, "SW": s_SW,
         }
         for name, b, t, alt in ORDER:
             steps[name](b, t, alt)

from contextlib import ExitStack

import concourse.mybir as mybir
from concourse.masks import make_identity

B, NS, NT, D, V = 4, 512, 512, 1024, 512
TEMPERATURE = 0.8
POWER = 0.8
FLOPS = 2 * B * NS * NT * (D + V)

F32 = mybir.dt.float32
BF16 = mybir.dt.bfloat16
I32 = mybir.dt.int32
U32 = mybir.dt.uint32
U8 = mybir.dt.uint8
FP8X4 = mybir.dt.float8_e4m3fn_x4
ALU = mybir.AluOpType
ACT = mybir.ActivationFunctionType

P = 128
PACK = 4
K_PASS = P * PACK
PASSES = D // K_PASS
HALF = 256
assert NS == NT == K_PASS

LOADS = [("yt",0), ("y",1), ("x",1), ("yt",1), ("yt",2), ("y",2), ("x",2), ("yt",3), ("y",3), ("x",3), ("ys",0), ("ys",1), ("ys",2), ("ys",3)]
ORDER = [
    ("Ty", 0, 0, 0), ("Ty", 0, 1, 0), ("Ty", 0, 2, 0), ("Ty", 0, 3, 0), ("Tx", 0, 0, 0),
    ("Tx", 0, 1, 0), ("Tx", 0, 2, 0), ("Tx", 0, 3, 0), ("Cy", 0, 0, 1), ("Cy", 0, 1, 1),
    ("Cy", 0, 2, 0), ("Cy", 0, 3, 0), ("Qy", 0, 0, 0), ("Qy", 0, 1, 0), ("Cx", 0, 0, 0),
    ("Cx", 0, 1, 0), ("Cx", 0, 2, 0), ("Qx", 0, 0, 0), ("Cx", 0, 3, 0), ("Qx", 0, 1, 0),
    ("M1", 0, 0, 0), ("M1", 0, 1, 0), ("M1", 0, 2, 0), ("M1", 0, 3, 0), ("Ty", 1, 0, 0),
    ("Ty", 1, 1, 0), ("Ty", 1, 2, 0), ("Ty", 1, 3, 0), ("YI", 0, 0, 1), ("YI", 0, 1, 1),
    ("QV", 0, 0, 0), ("E", 0, 0, 0), ("E", 0, 1, 0), ("E", 0, 2, 0), ("E", 0, 3, 0),
    ("Cy", 1, 0, 1), ("Cy", 1, 1, 1), ("Cy", 1, 2, 1), ("GA", 0, 0, 0), ("Cy", 1, 3, 0),
    ("KA", 0, 0, 1), ("KA", 0, 1, 0), ("KA", 0, 2, 0), ("KA", 0, 3, 0), ("Tx", 1, 0, 0),
    ("Tx", 1, 1, 0), ("Tx", 1, 2, 0), ("Tx", 1, 3, 0), ("YI", 1, 0, 1), ("Cx", 1, 0, 0),
    ("YI", 1, 1, 1), ("Cx", 1, 1, 0), ("Cx", 1, 2, 0), ("Cx", 1, 3, 0), ("TK", 0, 0, 0),
    ("TK", 0, 1, 0), ("TK", 0, 2, 0), ("TK", 0, 3, 0), ("Ty", 2, 0, 0), ("Ty", 2, 1, 0),
    ("Ty", 2, 2, 0), ("Ty", 2, 3, 0), ("YI", 2, 0, 1), ("YI", 2, 1, 1), ("CK", 0, 0, 0),
    ("CK", 0, 1, 0), ("CK", 0, 2, 0), ("Tx", 2, 0, 0), ("CK", 0, 3, 0), ("Tx", 2, 1, 0),
    ("Tx", 2, 2, 0), ("Tx", 2, 3, 0), ("Qy", 1, 0, 0), ("Qx", 1, 0, 0), ("Qy", 1, 1, 0),
    ("Qx", 1, 1, 0), ("Cx", 2, 0, 1), ("GB", 0, 0, 0), ("Cy", 2, 0, 0), ("Cx", 2, 1, 1),
    ("Cy", 2, 1, 0), ("Cy", 2, 2, 0), ("Cx", 2, 2, 1), ("Qx", 2, 0, 0), ("Cy", 2, 3, 0),
    ("Cx", 2, 3, 0), ("Qx", 2, 1, 0), ("M1", 1, 0, 0), ("M1", 1, 1, 0), ("M1", 1, 2, 0),
    ("M1", 1, 3, 0), ("QV", 2, 0, 0), ("Ty", 3, 0, 0), ("Ty", 3, 1, 0), ("Ty", 3, 2, 0),
    ("Ty", 3, 3, 0), ("Qy", 2, 0, 0), ("Qy", 2, 1, 0), ("M1", 2, 0, 0), ("M1", 2, 1, 0),
    ("M1", 2, 2, 0), ("M1", 2, 3, 0), ("TR", 0, 0, 1), ("TR", 0, 1, 1), ("TR", 0, 2, 0),
    ("TR", 0, 3, 0), ("E", 1, 0, 0), ("E", 1, 1, 0), ("E", 1, 2, 0), ("E", 1, 3, 0),
    ("GA", 1, 0, 0), ("Tx", 3, 0, 0), ("Tx", 3, 1, 0), ("Tx", 3, 2, 0), ("Tx", 3, 3, 0),
    ("QV", 1, 0, 0), ("TG", 0, 0, 0), ("TG", 0, 1, 0), ("TS", 0, 0, 0), ("Cy", 3, 0, 0),
    ("Cy", 3, 1, 0), ("Cy", 3, 2, 0), ("KA", 1, 0, 0), ("Cy", 3, 3, 0), ("E", 2, 0, 0),
    ("KA", 1, 1, 0), ("QT", 0, 0, 0), ("Qy", 3, 0, 0), ("KA", 1, 2, 0), ("E", 2, 1, 0),
    ("KA", 1, 3, 0), ("E", 2, 2, 0), ("QT", 0, 1, 0), ("Qy", 3, 1, 0), ("E", 2, 3, 0),
    ("Cx", 3, 0, 1), ("Cx", 3, 1, 0), ("Cx", 3, 2, 0), ("RS", 0, 0, 0), ("Cx", 3, 3, 0),
    ("TK", 1, 0, 0), ("TK", 1, 1, 0), ("TK", 1, 2, 0), ("TK", 1, 3, 0), ("Qx", 3, 0, 0),
    ("GA", 2, 0, 0), ("Qx", 3, 1, 0), ("CK", 1, 0, 0), ("CK", 1, 1, 0), ("CK", 1, 2, 0),
    ("CK", 1, 3, 0), ("M2", 0, 0, 0), ("M2", 0, 1, 0), ("M2", 0, 2, 0), ("M2", 0, 3, 0),
    ("M1", 3, 0, 0), ("M1", 3, 1, 0), ("M1", 3, 2, 0), ("M1", 3, 3, 0), ("KA", 2, 0, 1),
    ("KA", 2, 1, 1), ("KA", 2, 2, 1), ("KA", 2, 3, 0), ("O", 0, 0, 0), ("O", 0, 1, 0),
    ("O", 0, 2, 0), ("O", 0, 3, 0), ("GB", 1, 0, 0), ("E", 3, 0, 0), ("TK", 2, 0, 0),
    ("TK", 2, 1, 0), ("TK", 2, 2, 0), ("TK", 2, 3, 0), ("E", 3, 1, 0), ("E", 3, 2, 0),
    ("E", 3, 3, 0), ("TR", 1, 0, 0), ("TR", 1, 1, 0), ("TR", 1, 2, 0), ("TR", 1, 3, 0),
    ("YI", 3, 0, 1), ("YI", 3, 1, 1), ("TG", 1, 0, 0), ("TG", 1, 1, 0), ("TS", 1, 0, 0),
    ("CK", 2, 0, 0), ("CK", 2, 1, 0), ("CK", 2, 2, 0), ("RS", 1, 0, 1), ("CK", 2, 3, 0),
    ("QT", 1, 0, 0), ("QT", 1, 1, 0), ("GA", 3, 0, 0), ("KA", 3, 0, 1), ("KA", 3, 1, 1),
    ("KA", 3, 2, 0), ("GB", 2, 0, 0), ("KA", 3, 3, 0), ("M2", 1, 0, 0), ("M2", 1, 1, 0),
    ("M2", 1, 2, 0), ("M2", 1, 3, 0), ("SO", 0, 0, 0), ("SO", 0, 1, 0), ("SO", 0, 2, 0),
    ("SO", 0, 3, 0), ("O", 1, 0, 0), ("O", 1, 1, 0), ("O", 1, 2, 0), ("O", 1, 3, 0),
    ("SO", 1, 0, 0), ("SO", 1, 1, 0), ("SO", 1, 2, 0), ("SO", 1, 3, 0), ("TR", 2, 0, 0),
    ("TR", 2, 1, 0), ("TR", 2, 2, 0), ("TR", 2, 3, 0), ("QV", 3, 0, 0), ("TG", 2, 0, 0),
    ("OI", 0, 0, 1), ("TK", 3, 0, 0), ("TK", 3, 1, 0), ("TK", 3, 2, 0), ("TK", 3, 3, 0),
    ("CK", 3, 0, 0), ("TG", 2, 1, 0), ("CK", 3, 1, 0), ("CK", 3, 2, 0), ("CK", 3, 3, 0),
    ("OI", 0, 1, 1), ("GB", 3, 0, 0), ("QT", 2, 0, 0), ("QT", 2, 1, 0), ("TS", 2, 0, 0),
    ("QO", 0, 0, 0), ("QO", 0, 1, 0), ("RS", 2, 0, 1), ("M2", 2, 0, 0), ("M2", 2, 1, 0),
    ("M2", 2, 2, 0), ("M2", 2, 3, 0), ("TR", 3, 0, 1), ("TR", 3, 1, 1), ("TR", 3, 2, 1),
    ("TR", 3, 3, 1), ("TS", 3, 0, 0), ("O", 2, 0, 0), ("O", 2, 1, 0), ("O", 2, 2, 0),
    ("O", 2, 3, 0), ("TG", 3, 0, 0), ("TG", 3, 1, 0), ("QT", 3, 0, 0), ("QT", 3, 1, 0),
    ("OI", 1, 0, 1), ("M2", 3, 0, 0), ("M2", 3, 1, 0), ("M2", 3, 2, 0), ("M2", 3, 3, 0),
    ("OI", 1, 1, 1), ("QO", 1, 0, 0), ("QO", 1, 1, 0), ("SW", 0, 0, 0), ("SO", 2, 0, 0),
    ("SO", 2, 1, 0), ("SO", 2, 2, 0), ("SO", 2, 3, 0), ("SW", 0, 1, 0), ("RS", 3, 0, 1),
    ("OI", 2, 0, 1), ("SW", 1, 0, 0), ("O", 3, 0, 0), ("O", 3, 1, 0), ("O", 3, 2, 0),
    ("O", 3, 3, 0), ("OI", 2, 1, 1), ("SW", 1, 1, 0), ("SO", 3, 0, 0), ("SO", 3, 1, 0),
    ("SO", 3, 2, 0), ("SO", 3, 3, 0), ("OI", 3, 0, 1), ("OI", 3, 1, 0), ("QO", 2, 0, 0),
    ("QO", 2, 1, 0), ("QO", 3, 0, 0), ("QO", 3, 1, 0), ("SW", 2, 0, 0), ("SW", 2, 1, 0),
    ("SW", 3, 0, 0), ("SW", 3, 1, 0),
]


def tile_unbalancedsinkhorngainedsumdifference_kernel(tc, x, y, p, q, g, ys, yt, out_0, out_1, out_2):
    nc = tc.nc
    with ExitStack() as ctx:
        const = ctx.enter_context(tc.tile_pool(name="const", bufs=1))
        inputs = ctx.enter_context(tc.tile_pool(name="inputs", bufs=B))
        work = ctx.enter_context(tc.tile_pool(name="work", bufs=2))
        small = ctx.enter_context(tc.tile_pool(name="small", bufs=B))
        banks = ctx.enter_context(tc.psum_pool(name="banks", bufs=7))
        gain_bank = ctx.enter_context(tc.psum_pool(name="gain_bank", bufs=1))
        feats = ctx.enter_context(tc.tile_pool(name="feats", bufs=3))
        ctx.enter_context(tc.manual_schedule())

        st = [dict() for b in range(B)]
        sources = {"x": x, "y": y, "yt": yt, "ys": ys}

        def get(b, name, pool, shape, dtype):
            if name not in st[b]:
                st[b][name] = pool.tile(shape, dtype, name=name, align_bytes=64)
            return st[b][name]

        def load(name, b):
            rows = sources[name][b].rearrange("(p t) d -> p t d", t=PACK)
            dst = get(b, name, inputs if name in ("yt", "ys") else feats, [P, PACK, rows.shape[2]], BF16)
            step = PACK if name in ("yt", "ys") else (1 if b == 0 else 2)
            for t in range(0, PACK, step):
                nc.sync.dma_start(out=dst[:, t : t + step, :], in_=rows[:, t : t + step, :])

        ident = const.tile([P, P], F32)
        make_identity(nc, ident[:])
        neg_one = const.tile([P, PACK], F32)
        nc.gpsimd.memset(neg_one[:], -1.0)
        expo = const.tile([P, PACK], F32)
        nc.scalar.activation(out=expo[:], in_=neg_one[:], func=ACT.Copy, scale=POWER)
        load("y", 0)
        load("x", 0)
        pq = const.tile([P, 2, B, PACK], BF16)
        g_sb = const.tile([P, B, PACK], BF16)
        pq_inv = const.tile([P, 2, B, PACK], F32)
        nc.sync.dma_start(out=pq[:, 0], in_=p.rearrange("b (p t) -> p b t", t=PACK))
        nc.sync.dma_start(out=pq[:, 1], in_=q.rearrange("b (p t) -> p b t", t=PACK))
        nc.sync.dma_start(out=g_sb[:], in_=g.rearrange("b (p t) -> p b t", t=PACK))
        for name, b in LOADS:
            load(name, b)
        g_fac = const.tile([P, B * PACK], F32)
        nc.gpsimd.tensor_scalar(
            out=g_fac[:], in0=g_sb[:].rearrange("p b t -> p (b t)"), scalar1=-float(NT), scalar2=0.0, op0=ALU.mult, op1=ALU.add
        )
        gains = gain_bank.tile([P, B, PACK], F32)
        out_scales = const.tile([P, B * V], U8, align_bytes=64)

        def copy_on(alt, out, in_):
            if alt:
                nc.vector.tensor_copy(out=out, in_=in_)
            else:
                nc.scalar.copy(out=out, in_=in_)

        def turn(name, b, t):
            bank = banks.tile([P, PASSES, 2, P], F32, name="bank")
            st[b]["turned", name, t] = bank
            words = st[b][name][:, t, :].bitcast(F32)
            for c in range(PASSES):
                for u in range(2):
                    nc.tensor.transpose(bank[:, c, u, :], words[:, 256 * c + u : 256 * (c + 1) : 2], ident[:])

        def s_Ty(b, t, alt):
            turn("y", b, t)

        def s_Tx(b, t, alt):
            turn("x", b, t)

        def s_Cy(b, t, alt):
            yg = get(b, "yg", work, [P, PASSES, PACK, P * PACK], BF16)
            out = yg[:, :, t, :].bitcast(F32).rearrange("p c (r u) -> p c r u", u=2)
            copy_on(alt, out, st[b]["turned", "y", t][:].rearrange("p c u r -> p c r u"))

        def s_Cx(b, t, alt):
            xg = get(b, "xg", work, [P, PACK, PASSES, P * PACK], BF16)
            out = xg[:, t, :, :].bitcast(F32).rearrange("p c (r u) -> p c r u", u=2)
            copy_on(alt, out, st[b]["turned", "x", t][:].rearrange("p c u r -> p c r u"))

        def s_Qy(b, c, alt):
            codes = get(b, "yq", work, [P, PASSES, NT], U32)
            scales = get(b, "ysc", work, [P, PASSES, NT], U8)
            nc.vector.quantize_mx(
                out=codes[:, c, :].bitcast(FP8X4), scales=scales[:, c, :], in_=st[b]["yg"][:, c].rearrange("p t n -> p (t n)")
            )

        def s_Qx(b, h, alt):
            codes = get(b, "xq", work, [P, 2, 2 * PASSES * P], U32)
            scales = get(b, "xsc", work, [P, 2, 2 * PASSES * P], U8)
            nc.vector.quantize_mx(
                out=codes[:, h, :].bitcast(FP8X4),
                scales=scales[:, h, :],
                in_=st[b]["xg"][:, 2 * h : 2 * h + 2].rearrange("p t c n -> p (t c n)"),
            )
            if b == 0 and h == 1:
                nc.vector.reciprocal(out=pq_inv[:], in_=pq[:])
                nc.gpsimd.tensor_scalar(
                    out=pq_inv[:, 1], in0=pq_inv[:, 1], scalar1=-1.0, scalar2=0.0, op0=ALU.mult, op1=ALU.add
                )

        def s_M1(b, t, alt):
            s = st[b]
            bank = banks.tile([P, NT], F32, name="bank")
            s["score", t] = bank
            for c in range(PASSES):
                cols = slice(P * (PASSES * (t % 2) + c), P * (PASSES * (t % 2) + c + 1))
                nc.tensor.matmul_mx(
                    out=bank[:],
                    lhsT=s["xq"][:, t // 2, cols].bitcast(FP8X4),
                    lhsT_scale=s["xsc"][:, t // 2, cols],
                    rhs=s["yq"][:, c, :].bitcast(FP8X4),
                    rhs_scale=s["ysc"][:, c, :],
                    start=(c == 0),
                    stop=(c == PASSES - 1),
                )

        def s_E(b, t, alt):
            k = get(b, "k", work, [P, PACK, NT], F32)
            rs = get(b, "rs", small, [P, PACK], F32)
            nc.scalar.activation(
                out=k[:, t, :], in_=st[b]["score", t][:], func=ACT.Exp, scale=1.0 / TEMPERATURE, accum_out=rs[:, t : t + 1]
            )

        def s_GA(b, t, alt):
            ratio = get(b, "row_ratio", small, [P, PACK], F32)
            a = get(b, "a", small, [P, PACK], F32)
            nc.gpsimd.tensor_tensor(out=ratio[:], in0=st[b]["rs"][:], in1=pq_inv[:, 0, b, :], op=ALU.mult)
            nc.gpsimd.tensor_tensor(out=a[:], in0=ratio[:], in1=expo[:], op=ALU.pow)

        def s_KA(b, t, alt):
            s = st[b]
            if alt:
                nc.scalar.activation(out=s["k"][:, t, :], in_=s["k"][:, t, :], func=ACT.Copy, scale=s["a"][:, t : t + 1])
            else:
                nc.vector.tensor_scalar(
                    out=s["k"][:, t, :], in0=s["k"][:, t, :], scalar1=s["a"][:, t : t + 1], scalar2=None, op0=ALU.mult
                )

        def s_TK(b, tj, alt):
            if b == 0 and tj == 0:
                nc.tensor.matmul(out=gains[:].rearrange("p b t -> p (b t)"), lhsT=ident[:], rhs=g_fac[:], start=True, stop=True)
            bank = banks.tile([P, PACK, P], F32, name="bank")
            st[b]["kturned", tj] = bank
            for ti in range(PACK):
                nc.tensor.transpose(bank[:, ti, :], st[b]["k"][:, ti, P * tj : P * (tj + 1)], ident[:])

        def s_CK(b, tj, alt):
            kt = get(b, "kt", work, [P, PACK, NS], F32)
            cs = get(b, "cs", small, [P, PACK], F32)
            nc.scalar.activation(
                out=kt[:, tj, :],
                in_=st[b]["kturned", tj][:].rearrange("p t r -> p (t r)"),
                func=ACT.Copy,
                scale=-(NT ** (POWER - 1.0)),
                accum_out=cs[:, tj : tj + 1],
            )

        def s_GB(b, t, alt):
            ratio = get(b, "col_ratio", small, [P, PACK], F32)
            bb = get(b, "bb", small, [P, PACK], F32)
            nc.gpsimd.tensor_tensor(out=ratio[:], in0=st[b]["cs"][:], in1=pq_inv[:, 1, b, :], op=ALU.mult)
            nc.gpsimd.tensor_tensor(out=bb[:], in0=ratio[:], in1=expo[:], op=ALU.pow)

        def s_TR(b, t, alt):
            s = st[b]
            if alt:
                nc.scalar.activation(out=s["kt"][:, t, :], in_=s["kt"][:, t, :], func=ACT.Copy, scale=s["bb"][:, t : t + 1])
            else:
                nc.vector.tensor_scalar(
                    out=s["kt"][:, t, :], in0=s["kt"][:, t, :], scalar1=s["bb"][:, t : t + 1], scalar2=None, op0=ALU.mult
                )

        def s_TS(b, t, alt):
            bank = banks.tile([P, PACK, P], F32, name="bank")
            st[b]["partial"] = bank
            for ti in range(PACK):
                for tj in range(PACK):
                    nc.tensor.matmul(
                        out=bank[:, ti, :],
                        lhsT=st[b]["kt"][:, tj, P * ti : P * (ti + 1)],
                        rhs=ident[:],
                        start=(tj == 0),
                        stop=(tj == PACK - 1),
                        is_transpose=True,
                    )

        def s_RS(b, t, alt):
            m = get(b, "m", small, [P, PACK], F32)
            bank = st[b]["partial"]
            if alt:
                junk = get(b, "junk", small, [P, PACK, P], F32)
                for ti in range(PACK):
                    nc.scalar.activation(out=junk[:, ti, :], in_=bank[:, ti, :], func=ACT.Copy, accum_out=m[:, ti : ti + 1])
            else:
                nc.vector.tensor_reduce(out=m[:], in_=bank[:], axis=mybir.AxisListType.X, op=ALU.add)

        def s_TG(b, h, alt):
            tg = get(b, "tg", work, [P, NS, PACK], BF16)
            cols = slice(HALF * h, HALF * (h + 1))
            nc.vector.tensor_tensor(
                out=tg[:, cols, :],
                in0=st[b]["kt"][:, :, cols].rearrange("p t i -> p i t"),
                in1=gains[:, b, :].unsqueeze(1).to_broadcast([P, HALF, PACK]),
                op=ALU.mult,
            )

        def s_QT(b, h, alt):
            codes = get(b, "tq", work, [P, NS], U32)
            scales = get(b, "tsc", work, [P, NS], U8)
            cols = slice(HALF * h, HALF * (h + 1))
            nc.vector.quantize_mx(
                out=codes[:, cols].bitcast(FP8X4), scales=scales[:, cols], in_=st[b]["tg"][:, cols, :].rearrange("p n t -> p (n t)")
            )

        def s_YI(b, h, alt):
            s = st[b]
            get(b, "ytg", work, [P, V, PACK], BF16)
            cols = slice(HALF * h, HALF * (h + 1))
            copy_on(alt, s["ytg"][:, cols, :], s["yt"][:, :, cols].rearrange("p t v -> p v t"))

        def s_QV(b, t, alt):
            codes = get(b, "vq", small, [P, V], U32)
            scales = get(b, "vsc", small, [P, V], U8)
            nc.vector.quantize_mx(out=codes[:].bitcast(FP8X4), scales=scales[:], in_=st[b]["ytg"][:].rearrange("p n t -> p (n t)"))

        def s_M2(b, t, alt):
            s = st[b]
            bank = banks.tile([P, V], F32, name="bank")
            s["sum", t] = bank
            cols = slice(P * t, P * (t + 1))
            nc.tensor.matmul_mx(
                out=bank[:],
                lhsT=s["tq"][:, cols].bitcast(FP8X4),
                lhsT_scale=s["tsc"][:, cols],
                rhs=s["vq"][:].bitcast(FP8X4),
                rhs_scale=s["vsc"][:],
                start=True,
                stop=True,
            )

        def s_O(b, t, alt):
            s = st[b]
            o = get(b, "o", work, [P, PACK, V], F32)
            nc.vector.scalar_tensor_tensor(
                out=o[:, t, :], in0=s["ys"][:, t, :], scalar=s["m"][:, t : t + 1], in1=s["sum", t][:], op0=ALU.mult, op1=ALU.add
            )

        def s_SO(b, t, alt):
            rows = out_0[b].rearrange("(p t) v -> p t v", t=PACK)
            nc.sync.dma_start(out=rows[:, t, :], in_=st[b]["o"][:, t, :])

        def s_OI(b, h, alt):
            s = st[b]
            get(b, "og", work, [P, V, PACK], BF16)
            cols = slice(HALF * h, HALF * (h + 1))
            copy_on(not alt, s["og"][:, cols, :], s["o"][:, :, cols].rearrange("p t v -> p v t"))

        def s_QO(b, h, alt):
            codes = get(b, "oq", work, [P, V], U32)
            cols = slice(HALF * h, HALF * (h + 1))
            nc.vector.quantize_mx(
                out=codes[:, cols].bitcast(FP8X4),
                scales=out_scales[:, V * b + HALF * h : V * b + HALF * (h + 1)],
                in_=st[b]["og"][:, cols, :].rearrange("p n t -> p (n t)"),
            )

        def s_SW(b, h, alt):
            words = out_1[0].rearrange("p m t -> p (m t)").bitcast(I32)
            nc.sync.dma_start(
                out=words[:, V * b + HALF * h : V * b + HALF * (h + 1)], in_=st[b]["oq"][:, HALF * h : HALF * (h + 1)].bitcast(I32)
            )

        steps = {
            "Ty": s_Ty, "Tx": s_Tx, "Cy": s_Cy, "Cx": s_Cx, "Qy": s_Qy, "Qx": s_Qx, "M1": s_M1, "E": s_E, "GA": s_GA,
            "KA": s_KA, "TK": s_TK, "CK": s_CK, "GB": s_GB, "TR": s_TR, "TG": s_TG, "QT": s_QT, "YI": s_YI, "QV": s_QV,
            "TS": s_TS, "RS": s_RS, "M2": s_M2, "O": s_O, "SO": s_SO, "OI": s_OI, "QO": s_QO, "SW": s_SW,
        }
        for name, b, t, alt in ORDER:
            steps[name](b, t, alt)
        for quad in range(4):
            nc.scalar.dma_start(
                out=out_2[0, 4 * quad : 4 * quad + 4, :].bitcast(I32),
                in_=out_scales[32 * quad : 32 * quad + 4, :].bitcast(I32),
            )
